import numpy as np
CORES = [118,246,374,502,126,254,382,510]
N = 8
F = 512
def setup_inputs(rng):
    return {"a": rng.standard_normal((N, 128, N * 128), dtype=np.float32), "w": rng.standard_normal((N, 128, F), dtype=np.float32)}
def reference(a, w):
    tot = np.zeros((N * 128, F))
    for j in range(N):
        tot += a[j].astype(np.float64).T @ w[j].astype(np.float64)
    return {"y": np.stack([tot[128 * r:128 * r + 128] for r in range(N)]).astype(np.float32 if a.dtype != np.float64 else np.float64)}

@@ -1,0 +1,150 @@
+from concourse.mybir import AluOpType
+
+SCRATCH = {
+    "S": ("sbuf", [128, 768], "float32"),
+    "po": ("psum", [128, 512], "float32"),
+    "ph": ("psum", [128, 512], "float32"),
+}
+SEMAPHORES = ["il", "ta", "ta2", "vi1", "vi2", "tsent", "wl", "wa", "wsent", "lc", "lb0", "lb1", "uc", "ub0", "ub1",
+              "tmm", "vc", "ve", "va", "vf", "ba", "ca", "ssent", "csent", "bfree", "cfree", "wmfree", "crl", "ys"]
+
+NP = 4
+CW = 128
+
+
+def rank_program(g, core, T, topo):
+    rank = T.rank_of(core)
+    if rank is None:
+        return
+    sem = T.sem
+    S, po, ph = T.S, T.po, T.ph
+    grp, h = rank // 4, rank % 4
+    mate = T.cores[(1 - grp) * 4 + h]
+    peer = T.cores[grp * 4 + (h ^ 1)]
+    part = T.cores[grp * 4 + (3 - h)]
+    hD, hS, hC, hO = (h + 2) % 4, h ^ 1, 3 - h, h
+    order = [hD, hS, hC, hO]
+
+    TW, C, B0, B1, WO = S[:, 0:128], S[:, 128:256], S[:, 256:384], S[:, 384:512], S[:, 512:640]
+    WM = S[:, 640:768]
+    B, W2 = S[:, 256:512], S[:, 512:768]
+    tile_slot = [C, B0, B1, C]
+    tile_ld = [sem.lc, sem.lb0, sem.lb1, sem.lc]
+    tile_use = [sem.uc, sem.ub0, sem.ub1, sem.uc]
+
+    def send(dst, out_ap, in_ap, rsem, lsem):
+        rid, pid = topo.addr(dst, core)
+        g.remote_dma(out_ap, in_ap, rsem, lsem, pid, rid, 0xFF)
+
+    def signal(dst, rsem):
+        rid, pid = topo.addr(dst, core)
+        g.remote_sem_update(rsem, sem.crl, pid, rid, 0x01)
+
+    def own_tile(hidx):
+        blk = grp * 4 + hidx
+        return T.a[:, blk * 128:(blk + 1) * 128]
+
+    sy, sc, ve, te = g.sync, g.scalar, g.vector, g.tensor
+
+    mh = (1 - grp) * 512
+    sy.dma_start(S[:, 0:512], T.a[:, mh:mh + 512]).then_inc(sem.il, 16)
+    g.wait_ge(sem.il, 16)
+    send(mate, W2, S[:, 0:256], sem.ta, sem.tsent)
+    ve.wait_ge(sem.ta, 8)
+    ve.tensor_copy(ph[:, 0:256], W2).then_inc(sem.vi1, 1)
+    g.wait_ge(sem.vi1, 1)
+    g.wait_ge(sem.ta, 8)
+    send(mate, S[:, 0:256], B, sem.ta2, sem.tsent)
+    ve.wait_ge(sem.ta2, 8)
+    ve.tensor_copy(ph[:, 256:512], S[:, 0:256]).then_inc(sem.vi2, 1)
+
+    sy.wait_ge(sem.vi1, 1)
+    sy.dma_start(WO, T.w[:, 0:CW]).then_inc(sem.wl, 16)
+    sy.wait_ge(sem.tsent, 16)
+    sy.dma_start(B0, own_tile(hS)).then_inc(sem.lb0, 16)
+    sy.dma_start(B1, own_tile(hC)).then_inc(sem.lb1, 16)
+    sc.wait_ge(sem.vi2, 1)
+    sc.dma_start(C, own_tile(hD)).then_inc(sem.lc, 16)
+
+    ncred = 0
+    for f in range(NP):
+        last = f == NP - 1
+        g.wait_ge(sem.wl, 16 * (f + 1))
+        if f == 0:
+            g.wait_ge(sem.ta2, 8)
+        else:
+            g.wait_ge(sem.wmfree, f)
+        send(mate, WM, WO, sem.wa, sem.wsent)
+        g.wait_ge(sem.ub0, f + 1)
+        g.wait_ge(sem.ub1, f + 1)
+        signal(peer, sem.bfree)
+        g.wait_ge(sem.uc, 2 * f + 2)
+        signal(part, sem.cfree)
+        ncred += 2
+        g.wait_ge(sem.ve, f + 1)
+        g.wait_ge(sem.bfree, f + 1)
+        send(peer, B, W2, sem.ba, sem.ssent)
+        g.wait_ge(sem.va, f + 1)
+        g.wait_ge(sem.cfree, f + 1)
+        send(part, C, B0, sem.ca, sem.csent)
+        if not last:
+            g.wait_ge(sem.ssent, 8 * (f + 1))
+            signal(mate, sem.wmfree)
+            ncred += 1
+
+        lcn = [2 * f + 1, f + 1, f + 1, 2 * f + 2]
+        for k in range(4):
+            te.wait_ge(tile_ld[k], 16 * lcn[k])
+            if k == 0:
+                te.wait_ge(sem.wl, 16 * (f + 1))
+                if f > 0:
+                    te.wait_ge(sem.ve, f)
+                    te.wait_ge(sem.va, f)
+            reg = po[:, k * 128:(k + 1) * 128]
+            te.matmul(reg, tile_slot[k], WO, start=True, stop=False).then_inc(tile_use[k], 1)
+            te.wait_ge(sem.vc, 4 * f + k + 1)
+            if k == 0:
+                te.wait_ge(sem.wa, 8 * (f + 1))
+            te.matmul(reg, TW, WM, start=False, stop=True).then_inc(sem.tmm, 1)
+
+        for k in range(4):
+            if k == 0:
+                if f == 0:
+                    ve.wait_ge(sem.vi1, 1)
+                    ve.wait_ge(sem.vi2, 1)
+                else:
+                    ve.wait_ge(sem.ys, 16 * f)
+            else:
+                ve.wait_ge(sem.tmm, 4 * f + k)
+            hk = order[k]
+            ve.tensor_copy(TW, ph[:, hk * 128:(hk + 1) * 128]).then_inc(sem.vc, 1)
+        ve.wait_ge(sem.tmm, 4 * f + 4)
+        ve.wait_ge(sem.uc, 2 * f + 2)
+        ve.wait_ge(sem.ub0, f + 1)
+        ve.wait_ge(sem.ub1, f + 1)
+        ve.wait_ge(sem.wsent, 8 * (f + 1))
+        ve.tensor_copy(W2, po[:, 0:256]).then_inc(sem.ve, 1)
+        ve.wait_ge(sem.ba, 8 * (f + 1))
+        ve.tensor_tensor(B, po[:, 256:512], B, AluOpType.add).then_inc(sem.va, 1)
+        ve.wait_ge(sem.ca, 8 * (f + 1))
+        ve.wait_ge(sem.va, f + 1)
+        ve.tensor_tensor(TW, B1, C, AluOpType.add).then_inc(sem.vf, 1)
+
+        sc.wait_ge(sem.uc, 2 * f + 1)
+        sc.dma_start(C, own_tile(hO)).then_inc(sem.lc, 16)
+        sc.wait_ge(sem.vf, f + 1)
+        if not last:
+            sc.dma_start(C, own_tile(hD)).then_inc(sem.lc, 16)
+        sc.dma_start(T.y[:, f * CW:(f + 1) * CW], TW).then_inc(sem.ys, 16)
+        if not last:
+            sy.wait_ge(sem.ssent, 8 * (f + 1))
+            sy.dma_start(WO, T.w[:, (f + 1) * CW:(f + 2) * CW]).then_inc(sem.wl, 16)
+            sy.wait_ge(sem.csent, 8 * (f + 1))
+            sy.dma_start(B0, own_tile(hS)).then_inc(sem.lb0, 16)
+            sy.wait_ge(sem.vf, f + 1)
+            sy.dma_start(B1, own_tile(hC)).then_inc(sem.lb1, 16)
+
+    g.wait_ge(sem.ssent, 8 * NP)
+    g.wait_ge(sem.csent, 8 * NP)
+    g.wait_ge(sem.crl, ncred)
+    g.wait_ge(sem.ys, 16 * NP)

@@ -6,7 +6,8 @@ SCRATCH = {
     "ph": ("psum", [128, 512], "float32"),
 }
 SEMAPHORES = ["il", "ta", "ta2", "vi1", "vi2", "tsent", "wl", "wa", "wsent", "lc", "lb0", "lb1", "uc", "ub0", "ub1",
-              "tmm", "vc", "ve", "va", "vf", "ba", "ca", "ssent", "csent", "bfree", "cfree", "wmfree", "crl", "ys"]
+              "tmm", "vc", "ve", "va0", "va1", "vf", "ba0", "ba1", "ca", "dsent", "ssent", "csent", "bfree", "cfree",
+              "wmfree", "crl", "ys"]
 
 NP = 4
 CW = 128
@@ -25,9 +26,8 @@ def rank_program(g, core, T, topo):
     hD, hS, hC, hO = (h + 2) % 4, h ^ 1, 3 - h, h
     order = [hD, hS, hC, hO]
 
-    TW, C, B0, B1, WO = S[:, 0:128], S[:, 128:256], S[:, 256:384], S[:, 384:512], S[:, 512:640]
-    WM = S[:, 640:768]
-    B, W2 = S[:, 256:512], S[:, 512:768]
+    WM, WO, TW, C, B0, B1 = [S[:, i * 128:(i + 1) * 128] for i in range(6)]
+    STAGE = S[:, 128:384]
     tile_slot = [C, B0, B1, C]
     tile_ld = [sem.lc, sem.lb0, sem.lb1, sem.lc]
     tile_use = [sem.uc, sem.ub0, sem.ub1, sem.uc]
@@ -47,16 +47,16 @@ def rank_program(g, core, T, topo):
     sy, sc, ve, te = g.sync, g.scalar, g.vector, g.tensor
 
     mh = (1 - grp) * 512
-    sy.dma_start(S[:, 0:512], T.a[:, mh:mh + 512]).then_inc(sem.il, 16)
+    sy.dma_start(S[:, 256:768], T.a[:, mh:mh + 512]).then_inc(sem.il, 16)
     g.wait_ge(sem.il, 16)
-    send(mate, W2, S[:, 0:256], sem.ta, sem.tsent)
+    send(mate, S[:, 0:256], S[:, 256:512], sem.ta, sem.tsent)
     ve.wait_ge(sem.ta, 8)
-    ve.tensor_copy(ph[:, 0:256], W2).then_inc(sem.vi1, 1)
+    ve.tensor_copy(ph[:, 0:256], S[:, 0:256]).then_inc(sem.vi1, 1)
     g.wait_ge(sem.vi1, 1)
     g.wait_ge(sem.ta, 8)
-    send(mate, S[:, 0:256], B, sem.ta2, sem.tsent)
+    send(mate, S[:, 256:512], S[:, 512:768], sem.ta2, sem.tsent)
     ve.wait_ge(sem.ta2, 8)
-    ve.tensor_copy(ph[:, 256:512], S[:, 0:256]).then_inc(sem.vi2, 1)
+    ve.tensor_copy(ph[:, 256:512], S[:, 256:512]).then_inc(sem.vi2, 1)
 
     sy.wait_ge(sem.vi1, 1)
     sy.dma_start(WO, T.w[:, 0:CW]).then_inc(sem.wl, 16)
@@ -78,19 +78,21 @@ def rank_program(g, core, T, topo):
         g.wait_ge(sem.ub0, f + 1)
         g.wait_ge(sem.ub1, f + 1)
         signal(peer, sem.bfree)
-        g.wait_ge(sem.uc, 2 * f + 2)
-        signal(part, sem.cfree)
-        ncred += 2
+        ncred += 1
         g.wait_ge(sem.ve, f + 1)
         g.wait_ge(sem.bfree, f + 1)
-        send(peer, B, W2, sem.ba, sem.ssent)
-        g.wait_ge(sem.va, f + 1)
-        g.wait_ge(sem.cfree, f + 1)
-        send(part, C, B0, sem.ca, sem.csent)
+        send(peer, B0, WO, sem.ba0, sem.dsent)
+        send(peer, B1, TW, sem.ba1, sem.ssent)
         if not last:
-            g.wait_ge(sem.ssent, 8 * (f + 1))
+            g.wait_ge(sem.tmm, 4 * f + 4)
             signal(mate, sem.wmfree)
             ncred += 1
+        g.wait_ge(sem.uc, 2 * f + 2)
+        signal(part, sem.cfree)
+        ncred += 1
+        g.wait_ge(sem.va0, f + 1)
+        g.wait_ge(sem.cfree, f + 1)
+        send(part, C, B0, sem.ca, sem.csent)
 
         lcn = [2 * f + 1, f + 1, f + 1, 2 * f + 2]
         for k in range(4):
@@ -99,7 +101,8 @@ def rank_program(g, core, T, topo):
                 te.wait_ge(sem.wl, 16 * (f + 1))
                 if f > 0:
                     te.wait_ge(sem.ve, f)
-                    te.wait_ge(sem.va, f)
+                    te.wait_ge(sem.va0, f)
+                    te.wait_ge(sem.va1, f)
             reg = po[:, k * 128:(k + 1) * 128]
             te.matmul(reg, tile_slot[k], WO, start=True, stop=False).then_inc(tile_use[k], 1)
             te.wait_ge(sem.vc, 4 * f + k + 1)
@@ -123,11 +126,14 @@ def rank_program(g, core, T, topo):
         ve.wait_ge(sem.ub0, f + 1)
         ve.wait_ge(sem.ub1, f + 1)
         ve.wait_ge(sem.wsent, 8 * (f + 1))
-        ve.tensor_copy(W2, po[:, 0:256]).then_inc(sem.ve, 1)
-        ve.wait_ge(sem.ba, 8 * (f + 1))
-        ve.tensor_tensor(B, po[:, 256:512], B, AluOpType.add).then_inc(sem.va, 1)
+        ve.tensor_copy(STAGE, po[:, 0:256]).then_inc(sem.ve, 1)
+        ve.wait_ge(sem.ba0, 8 * (f + 1))
+        ve.tensor_tensor(B0, po[:, 256:384], B0, AluOpType.add).then_inc(sem.va0, 1)
+        ve.wait_ge(sem.ba1, 8 * (f + 1))
+        ve.tensor_tensor(B1, po[:, 384:512], B1, AluOpType.add).then_inc(sem.va1, 1)
         ve.wait_ge(sem.ca, 8 * (f + 1))
-        ve.wait_ge(sem.va, f + 1)
+        ve.wait_ge(sem.va1, f + 1)
+        ve.wait_ge(sem.ssent, 8 * (f + 1))
         ve.tensor_tensor(TW, B1, C, AluOpType.add).then_inc(sem.vf, 1)
 
         sc.wait_ge(sem.uc, 2 * f + 1)
@@ -137,14 +143,14 @@ def rank_program(g, core, T, topo):
             sc.dma_start(C, own_tile(hD)).then_inc(sem.lc, 16)
         sc.dma_start(T.y[:, f * CW:(f + 1) * CW], TW).then_inc(sem.ys, 16)
         if not last:
-            sy.wait_ge(sem.ssent, 8 * (f + 1))
+            sy.wait_ge(sem.dsent, 8 * (f + 1))
             sy.dma_start(WO, T.w[:, (f + 1) * CW:(f + 2) * CW]).then_inc(sem.wl, 16)
             sy.wait_ge(sem.csent, 8 * (f + 1))
             sy.dma_start(B0, own_tile(hS)).then_inc(sem.lb0, 16)
             sy.wait_ge(sem.vf, f + 1)
             sy.dma_start(B1, own_tile(hC)).then_inc(sem.lb1, 16)
 
-    g.wait_ge(sem.ssent, 8 * NP)
+    g.wait_ge(sem.dsent, 8 * NP)
     g.wait_ge(sem.csent, 8 * NP)
     g.wait_ge(sem.crl, ncred)
     g.wait_ge(sem.ys, 16 * NP)

from concourse.mybir import AluOpType

SCRATCH = {
    "S": ("sbuf", [128, 768], "float32"),
    "po": ("psum", [128, 512], "float32"),
    "ph": ("psum", [128, 512], "float32"),
}
SEMAPHORES = ["il", "ta", "ta2", "vi1", "vi2", "tsent", "wl", "wa", "wsent", "lc", "lb0", "lb1", "uc", "ub0", "ub1",
              "tmm", "vc", "ve", "va0", "va1", "vf", "ba0", "ba1", "ca", "dsent", "ssent", "csent", "bfree", "cfree",
              "wmfree", "crl", "ys"]

NP = 4
CW = 128


def rank_program(g, core, T, topo):
    rank = T.rank_of(core)
    if rank is None:
        return
    sem = T.sem
    S, po, ph = T.S, T.po, T.ph
    grp, h = rank // 4, rank % 4
    mate = T.cores[(1 - grp) * 4 + h]
    peer = T.cores[grp * 4 + (h ^ 1)]
    part = T.cores[grp * 4 + (3 - h)]
    hD, hS, hC, hO = (h + 2) % 4, h ^ 1, 3 - h, h
    order = [hD, hS, hC, hO]

    WM, WO, TW, C, B0, B1 = [S[:, i * 128:(i + 1) * 128] for i in range(6)]
    STAGE = S[:, 128:384]
    tile_slot = [C, B0, B1, C]
    tile_ld = [sem.lc, sem.lb0, sem.lb1, sem.lc]
    tile_use = [sem.uc, sem.ub0, sem.ub1, sem.uc]

    def send(dst, out_ap, in_ap, rsem, lsem):
        rid, pid = topo.addr(dst, core)
        g.remote_dma(out_ap, in_ap, rsem, lsem, pid, rid, 0xFF)

    def signal(dst, rsem):
        rid, pid = topo.addr(dst, core)
        g.remote_sem_update(rsem, sem.crl, pid, rid, 0x01)

    def own_tile(hidx):
        blk = grp * 4 + hidx
        return T.a[:, blk * 128:(blk + 1) * 128]

    sy, sc, ve, te = g.sync, g.scalar, g.vector, g.tensor

    mh = (1 - grp) * 512
    sy.dma_start(S[:, 256:768], T.a[:, mh:mh + 512]).then_inc(sem.il, 16)
    g.wait_ge(sem.il, 16)
    send(mate, S[:, 0:256], S[:, 256:512], sem.ta, sem.tsent)
    ve.wait_ge(sem.ta, 8)
    ve.tensor_copy(ph[:, 0:256], S[:, 0:256]).then_inc(sem.vi1, 1)
    g.wait_ge(sem.vi1, 1)
    g.wait_ge(sem.ta, 8)
    send(mate, S[:, 256:512], S[:, 512:768], sem.ta2, sem.tsent)
    ve.wait_ge(sem.ta2, 8)
    ve.tensor_copy(ph[:, 256:512], S[:, 256:512]).then_inc(sem.vi2, 1)

    sy.wait_ge(sem.vi1, 1)
    sy.dma_start(WO, T.w[:, 0:CW]).then_inc(sem.wl, 16)
    sy.wait_ge(sem.tsent, 16)
    sy.dma_start(B0, own_tile(hS)).then_inc(sem.lb0, 16)
    sy.dma_start(B1, own_tile(hC)).then_inc(sem.lb1, 16)
    sc.wait_ge(sem.vi2, 1)
    sc.dma_start(C, own_tile(hD)).then_inc(sem.lc, 16)

    ncred = 0
    for f in range(NP):
        last = f == NP - 1
        g.wait_ge(sem.wl, 16 * (f + 1))
        if f == 0:
            g.wait_ge(sem.ta2, 8)
        else:
            g.wait_ge(sem.wmfree, f)
        send(mate, WM, WO, sem.wa, sem.wsent)
        g.wait_ge(sem.ub0, f + 1)
        g.wait_ge(sem.ub1, f + 1)
        signal(peer, sem.bfree)
        ncred += 1
        g.wait_ge(sem.ve, f + 1)
        g.wait_ge(sem.bfree, f + 1)
        send(peer, B0, WO, sem.ba0, sem.dsent)
        send(peer, B1, TW, sem.ba1, sem.ssent)
        if not last:
            g.wait_ge(sem.tmm, 4 * f + 4)
            signal(mate, sem.wmfree)
            ncred += 1
        g.wait_ge(sem.uc, 2 * f + 2)
        signal(part, sem.cfree)
        ncred += 1
        g.wait_ge(sem.va0, f + 1)
        g.wait_ge(sem.cfree, f + 1)
        send(part, C, B0, sem.ca, sem.csent)

        lcn = [2 * f + 1, f + 1, f + 1, 2 * f + 2]
        for k in range(4):
            te.wait_ge(tile_ld[k], 16 * lcn[k])
            if k == 0:
                te.wait_ge(sem.wl, 16 * (f + 1))
                if f > 0:
                    te.wait_ge(sem.ve, f)
                    te.wait_ge(sem.va0, f)
                    te.wait_ge(sem.va1, f)
            reg = po[:, k * 128:(k + 1) * 128]
            te.matmul(reg, tile_slot[k], WO, start=True, stop=False).then_inc(tile_use[k], 1)
            te.wait_ge(sem.vc, 4 * f + k + 1)
            if k == 0:
                te.wait_ge(sem.wa, 8 * (f + 1))
            te.matmul(reg, TW, WM, start=False, stop=True).then_inc(sem.tmm, 1)

        for k in range(4):
            if k == 0:
                if f == 0:
                    ve.wait_ge(sem.vi1, 1)
                    ve.wait_ge(sem.vi2, 1)
                else:
                    ve.wait_ge(sem.ys, 16 * f)
            else:
                ve.wait_ge(sem.tmm, 4 * f + k)
            hk = order[k]
            ve.tensor_copy(TW, ph[:, hk * 128:(hk + 1) * 128]).then_inc(sem.vc, 1)
        ve.wait_ge(sem.tmm, 4 * f + 4)
        ve.wait_ge(sem.uc, 2 * f + 2)
        ve.wait_ge(sem.ub0, f + 1)
        ve.wait_ge(sem.ub1, f + 1)
        ve.wait_ge(sem.wsent, 8 * (f + 1))
        ve.tensor_copy(STAGE, po[:, 0:256]).then_inc(sem.ve, 1)
        ve.wait_ge(sem.ba0, 8 * (f + 1))
        ve.tensor_tensor(B0, po[:, 256:384], B0, AluOpType.add).then_inc(sem.va0, 1)
        ve.wait_ge(sem.ba1, 8 * (f + 1))
        ve.tensor_tensor(B1, po[:, 384:512], B1, AluOpType.add).then_inc(sem.va1, 1)
        ve.wait_ge(sem.ca, 8 * (f + 1))
        ve.wait_ge(sem.va1, f + 1)
        ve.wait_ge(sem.ssent, 8 * (f + 1))
        ve.tensor_tensor(TW, B1, C, AluOpType.add).then_inc(sem.vf, 1)

        sc.wait_ge(sem.uc, 2 * f + 1)
        sc.dma_start(C, own_tile(hO)).then_inc(sem.lc, 16)
        sc.wait_ge(sem.vf, f + 1)
        if not last:
            sc.dma_start(C, own_tile(hD)).then_inc(sem.lc, 16)
        sc.dma_start(T.y[:, f * CW:(f + 1) * CW], TW).then_inc(sem.ys, 16)
        if not last:
            sy.wait_ge(sem.dsent, 8 * (f + 1))
            sy.dma_start(WO, T.w[:, (f + 1) * CW:(f + 2) * CW]).then_inc(sem.wl, 16)
            sy.wait_ge(sem.csent, 8 * (f + 1))
            sy.dma_start(B0, own_tile(hS)).then_inc(sem.lb0, 16)
            sy.wait_ge(sem.vf, f + 1)
            sy.dma_start(B1, own_tile(hC)).then_inc(sem.lb1, 16)

    g.wait_ge(sem.dsent, 8 * NP)
    g.wait_ge(sem.csent, 8 * NP)
    g.wait_ge(sem.crl, ncred)
    g.wait_ge(sem.ys, 16 * NP)
